import numpy as np
import ml_dtypes


def mxq(x, axis, fmt="e4m3"):
    dtype, down = {"e4m3": (ml_dtypes.float8_e4m3fn, 7), "e5m2": (ml_dtypes.float8_e5m2, 14)}[fmt]
    v = np.moveaxis(np.asarray(x, np.float32).astype(ml_dtypes.bfloat16).astype(np.float64), axis, -1)
    blocks = v.reshape(v.shape[:-1] + (-1, 32))
    amax = np.abs(blocks).max(-1, keepdims=True)
    byte = np.maximum(np.where(amax > 0, np.frexp(amax)[1] - 1 + 127, 0) - down, 1)
    scale = np.exp2(byte - 127.0)
    codes = (blocks / scale).astype(np.float32).astype(dtype).astype(np.float64)
    return np.moveaxis((codes * scale).reshape(v.shape), -1, axis)


WIDE = False


def mx_kscale(k):
    if not WIDE:
        return np.ones(k)
    levels = np.array([18, -18])
    if k % 512:
        return np.exp2(np.random.permutation(np.resize(levels, k // 32))).repeat(32)
    a = np.empty((k // 512, 16))
    for p in range(k // 512):
        a[p, :8] = np.random.permutation(np.resize(levels, 8))
        for g in range(8):
            far = levels[np.abs(levels - a[p, g]) >= 10]
            a[p, g + 8] = far[np.random.randint(len(far))]
    return np.exp2(a.ravel()).repeat(32)


def f64(x):
    return np.asarray(x).astype(np.float64)


def striped(idx):
    return np.tile(np.asarray(idx).reshape(-1, 16).T, (8, 1)).astype(np.uint16)


def unstriped(offs):
    return offs[:16].T.reshape(-1).astype(np.int64)


B, N, T, D, DV = 2, 512, 2048, 512, 512


def setup_inputs():
    n = np.random.standard_normal
    idx = np.random.permutation(T)[:B * N]
    u = np.ones(T)
    u[idx] = mx_kscale(B * N)
    v = mx_kscale(DV)[:, None]
    coarse = lambda x: x.astype(np.float32).astype(ml_dtypes.bfloat16).astype(np.float64)
    r = np.random.randint(8, 33, T) / 16.0 * u
    return {
        "xT": (n((D, T)) / np.sqrt(N) / u).astype(np.float32),
        "dyT": (coarse(n((DV, T))) * v).astype(np.float32),
        "hT": coarse(n((DV, T))).astype(np.float32),
        "ts": np.tile(r, (128, 1)).astype(np.float32),
        "wm": (n((B, DV, D)) / np.sqrt(DV) / v).astype(np.float32),
        "offs": striped(idx),
    }


def reference(xT, dyT, hT, ts, wm, offs):
    idx = unstriped(offs)
    pick = lambda x: x[:, idx].reshape(x.shape[0], B, N).transpose(1, 0, 2)
    h = pick(f64(hT))
    dz = pick(f64(ts))[:, :1, :] * pick(f64(dyT)) * 2.0 * np.maximum(h, 0.0)
    gw = mxq(pick(f64(xT)), 2, "e4m3") @ mxq(dz, 2, "e5m2").transpose(0, 2, 1)
    dx = mxq(f64(wm), 1, "e4m3").transpose(0, 2, 1) @ mxq(dz, 1, "e5m2")
    gx = np.zeros((D, T))
    gx[:, idx] = dx.transpose(1, 0, 2).reshape(D, B * N)
    return gw, gx

@@ -1,0 +1,316 @@
+from contextlib import ExitStack
+
+import concourse.mybir as mybir
+from concourse.masks import make_identity
+
+B, N, T, D, DV = 2, 512, 2048, 512, 512
+FLOPS = 2 * B * N * D * DV * 2
+BYTES = 4 * (D * T + 2 * DV * T + T + B * DV * D + B * D * DV + D * T) + 2 * 128 * 64
+
+F32 = mybir.dt.float32
+BF16 = mybir.dt.bfloat16
+U32 = mybir.dt.uint32
+U16 = mybir.dt.uint16
+U8 = mybir.dt.uint8
+E4 = mybir.dt.float8_e4m3fn_x4
+E5 = mybir.dt.float8_e5m2_x4
+ACT = mybir.ActivationFunctionType
+MULT = mybir.AluOpType.mult
+ADD = mybir.AluOpType.add
+MAX = mybir.AluOpType.max
+P = 128
+
+
+def tile_attend_gex_wx_kernel(tc, xT, dyT, hT, ts, wm, offs, out_0, out_1):
+    nc = tc.nc
+    with ExitStack() as ctx:
+        lists = ctx.enter_context(tc.tile_pool(name="lists", bufs=1))
+        sb = ctx.enter_context(tc.tile_pool(name="sb", bufs=1))
+        ps = ctx.enter_context(tc.psum_pool(name="ps", bufs=1))
+
+        def tile(cols, dtype, name, tag=None, bufs=1):
+            return sb.tile([P, cols], dtype, name=name, tag=tag or name, bufs=bufs, align_bytes=64)
+
+        def bank(index, name):
+            return ps.tile([P, 512], F32, name=name, tag="bank%d" % index)
+
+        def move(engine, dst, src):
+            if engine == "S":
+                nc.scalar.copy(dst, src)
+            elif engine == "V":
+                nc.vector.tensor_copy(dst, src)
+            else:
+                nc.gpsimd.tensor_scalar(dst, src, 1.0, 0.0, MULT, ADD)
+
+        offsets = lists.tile([P, B * N // 16], U16, name="offsets")
+        nc.sync.dma_start(offsets[:], offs)
+        slots = [offsets[:, 32 * b : 32 * b + 32] for b in range(B)]
+
+        ident = tile(P, F32, "ident")
+        make_identity(nc, ident[:])
+
+        h_rows = hT.rearrange("(p j) t -> j p t", j=4)
+        dy_rows = dyT.rearrange("(p j) t -> j p t", j=4)
+        h_win = [tile(T, F32, "h%d" % j, tag="big%d" % (2 * j)) for j in range(4)]
+        dy_win = [tile(T, F32, "dy%d" % j, tag="big%d" % (2 * j + 1)) for j in range(4)]
+        ts_win = tile(T, F32, "ts_win")
+        gx_win = [tile(T, F32, "gx%d" % k) for k in range(4)]
+        w_raw, w_q, x_raw, h_g, a_g, dz_turned, dzn_q, dzi_q, x_q, x_turned = [{} for n in range(10)]
+        planes, dx_sb = {}, {}
+        dz = [tile(2048, BF16, "dz%d" % b) for b in range(B)]
+        dz_n = [tile(2048, BF16, "dz_n%d" % b) for b in range(B)]
+        dz_i = [tile(2048, BF16, "dz_i%d" % b) for b in range(B)]
+        x_i = {}
+        ts2 = [tile(N, F32, "ts2_%d" % b) for b in range(B)]
+
+        def load_ts():
+            nc.sync.dma_start(ts_win[:], ts)
+
+        def load_h(j):
+            nc.sync.dma_start(h_win[j][:], h_rows[j])
+
+        def load_dy(j):
+            nc.sync.dma_start(dy_win[j][:], dy_rows[j])
+
+        def load_w(b, half):
+            w_raw[b, half] = tile(1024, F32, "w_raw%d%d" % (b, half))
+            nc.sync.dma_start(
+                w_raw[b, half][:].rearrange("p (j d) -> p j d", j=4),
+                wm[b].rearrange("(p j) d -> p j d", j=4)[:, :, 256 * half : 256 * half + 256],
+            )
+
+        def load_x(c, tag=None):
+            x_raw[c] = tile(T, F32, "x_raw%d" % c, tag=tag)
+            nc.sync.dma_start(x_raw[c][:], xT[P * c : P * c + P, :])
+
+        def quantize(src, cols, dtype, name):
+            codes = tile(cols, U32, name + "_codes")
+            scales = tile(cols, U8, name + "_scales")
+            nc.vector.quantize_mx(out=codes[:].bitcast(dtype), scales=scales[:], in_=src[:])
+            return codes, scales
+
+        def gather_ts(b):
+            nc.vector.tensor_scalar(ts2[b][:], ts_win[:].indirect(slots[b]), 2.0, 0.0, MULT, ADD)
+
+        def prepare_w(b, half, engine="S"):
+            woven = tile(1024, BF16, "w_woven%d%d" % (b, half))
+            move(
+                engine,
+                woven[:].rearrange("p (c i j) -> p c j i", i=4, j=4),
+                w_raw[b, half][:].rearrange("p (j c i) -> p c j i", j=4, i=4),
+            )
+            w_q[b, half] = quantize(woven, 256, E4, "w%d%d" % (b, half))
+
+        def gather_h(j, b, tag="h_g", bufs=2):
+            h_g[j, b] = tile(N, F32, "h_g%d%d" % (j, b), tag=tag, bufs=bufs)
+            nc.vector.tensor_copy(h_g[j, b][:], h_win[j][:].indirect(slots[b]))
+
+        def gather_dy(j, b, tag="a_g", bufs=2):
+            a_g[j, b] = tile(N, F32, "a_g%d%d" % (j, b), tag=tag, bufs=bufs)
+            nc.vector.tensor_tensor(a_g[j, b][:], dy_win[j][:].indirect(slots[b]), ts2[b][:], MULT)
+
+        def form_dz(j, b):
+            plane = dz[b][:, N * j : N * j + N]
+            nc.vector.scalar_tensor_tensor(plane, h_g[j, b][:], 0.0, a_g[j, b][:], MAX, MULT)
+            u, e = divmod(j, 2)
+            if e == 0:
+                dz_turned[u, b] = bank(2 * b + u, "dz_turned%d%d" % (u, b))
+            for v in range(2):
+                c0 = 256 * v + P * e
+                nc.tensor.transpose(dz_turned[u, b][:, c0 : c0 + P], plane.bitcast(F32)[:, v : N // 2 : 2], ident[:])
+
+        def weave_words(dst, turned, u, engine="S"):
+            move(
+                engine,
+                dst[:, 1024 * u : 1024 * u + 1024].bitcast(F32).rearrange("s (c v) -> s c v", v=2),
+                turned[:].rearrange("s (v c) -> s c v", v=2),
+            )
+
+        def weave_dz_i(u, b):
+            weave_words(dz_i[b], dz_turned[u, b], u)
+
+        def weave_x(u, b, tag=None):
+            if u == 0:
+                x_i[b] = tile(2048, BF16, "x_i%d" % b, tag=tag)
+            weave_words(x_i[b], x_turned[u, b], u)
+
+        def weave_dz_n_pair(u, b, engine="S"):
+            move(
+                engine,
+                dz_n[b][:].rearrange("p (c i u e) -> p u c e i", i=4, u=2, e=2)[:, u],
+                dz[b][:, 1024 * u : 1024 * u + 1024].rearrange("p (e c i) -> p c e i", e=2, i=4),
+            )
+
+        def weave_dz_n(b, q, engine="S", parts=2):
+            move(
+                engine,
+                dz_n[b][:].rearrange("p (q c i j) -> p q c j i", q=parts, i=4, j=4)[:, q],
+                dz[b][:].rearrange("p (j q c i) -> p q c j i", j=4, q=parts, i=4)[:, q],
+            )
+
+        def q_dzn(b):
+            dzn_q[b] = quantize(dz_n[b], 512, E5, "dzn%d" % b)
+
+        def product(acc, lhs, c0, rhs):
+            nc.tensor.matmul_mx(
+                out=acc[:],
+                lhsT=lhs[0][:, c0 : c0 + P].bitcast(E4),
+                lhsT_scale=lhs[1][:, c0 : c0 + P],
+                rhs=rhs[0][:].bitcast(E5),
+                rhs_scale=rhs[1][:],
+                start=True,
+                stop=True,
+            )
+
+        def dx_block(k, b, engine="S", tag=None):
+            dx_sb[k, b] = tile(N, F32, "dx_sb%d%d" % (k, b), tag=tag)
+            acc = bank(6 + k % 2, "dx%d%d" % (k, b))
+            product(acc, w_q[b, k // 2], P * (k % 2), dzn_q[b])
+            move(engine, dx_sb[k, b][:], acc[:])
+
+        def scatter(k, b):
+            nc.vector.tensor_copy(gx_win[k][:].indirect(slots[b]), dx_sb[k, b][:])
+
+        def dx_scatter(k, b, engine="S", tag=None):
+            dx_block(k, b, engine, tag)
+            scatter(k, b)
+
+        def store_gx(k):
+            nc.sync.dma_start(out_1[P * k : P * k + P, :], gx_win[k][:])
+
+        def cast_x(c, engine="S", tag=None):
+            planes[c] = tile(T, BF16, "x_plane%d" % c, tag=tag)
+            for half in range(2):
+                cols = slice(1024 * half, 1024 * half + 1024)
+                if engine == "S":
+                    nc.scalar.activation(planes[c][:, cols], x_raw[c][:, cols], ACT.Copy)
+                else:
+                    nc.gpsimd.tensor_copy(planes[c][:, cols], x_raw[c][:, cols])
+
+        def gather_x(c, b, engine="S"):
+            x_g = tile(N, BF16, "x_g%d%d" % (c, b))
+            if engine == "S":
+                nc.scalar.activation(x_g[:], planes[c][:].indirect(slots[b]), ACT.Copy)
+            else:
+                nc.vector.tensor_copy(x_g[:], x_raw[c][:].indirect(slots[b]))
+            u, e = divmod(c, 2)
+            if e == 0:
+                x_turned[u, b] = bank(4 + b, "x_turned%d%d" % (u, b))
+            for v in range(2):
+                c0 = 256 * v + P * e
+                nc.tensor.transpose(x_turned[u, b][:, c0 : c0 + P], x_g[:].bitcast(F32)[:, v : N // 2 : 2], ident[:])
+
+        def q_dzi(b):
+            dzi_q[b] = quantize(dz_i[b], 512, E5, "dzi%d" % b)
+
+        def q_x(b):
+            x_q[b] = quantize(x_i[b], 512, E4, "x%d" % b)
+
+        def gw_blocks(b, c2, tag, engines="SS"):
+            gw = tile(2 * DV, F32, "gw_sb%d%d" % (b, c2), tag=tag)
+            for c in range(2):
+                acc = bank(2 * c2 + c, "gw%d%d%d" % (b, c2, c))
+                product(acc, x_q[b], P * (2 * c2 + c), dzi_q[b])
+                move(
+                    engines[c],
+                    gw[:, DV * c : DV * c + DV].rearrange("d (p j) -> d p j", j=4),
+                    acc[:].rearrange("d (j p) -> d p j", j=4),
+                )
+            nc.scalar.dma_start(
+                out_0[b, 256 * c2 : 256 * c2 + 256, :].rearrange("(c d) n -> d c n", c=2),
+                gw[:].rearrange("d (c n) -> d c n", c=2),
+            )
+
+        load_h(0)
+        load_ts()
+        load_dy(0)
+        load_x(0)
+        load_h(1)
+        load_dy(1)
+        load_x(1)
+        load_h(2)
+        load_dy(2)
+        load_h(3)
+        load_dy(3)
+        load_w(0, 0)
+        load_w(1, 0)
+        load_x(2, "big0")
+        load_x(3, "big1")
+        load_w(0, 1)
+        load_w(1, 1)
+        for k in range(4):
+            nc.vector.memset(gx_win[k][:], 0.0)
+        gather_h(0, 0)
+        gather_h(0, 1)
+        gather_ts(0)
+        gather_ts(1)
+        for j in range(2):
+            if j > 0:
+                gather_h(j, 0)
+                gather_h(j, 1)
+            gather_dy(j, 0)
+            gather_dy(j, 1)
+            form_dz(j, 0)
+            form_dz(j, 1)
+        gather_h(2, 0)
+        gather_h(2, 1, "h_g21", 1)
+        gather_dy(2, 0)
+        form_dz(2, 0)
+        gather_h(3, 0)
+        gather_h(3, 1)
+        gather_dy(3, 0)
+        form_dz(3, 0)
+        gather_dy(2, 1, "ts2_0", 1)
+        form_dz(2, 1)
+        cast_x(0)
+        gather_x(0, 0)
+        gather_x(0, 1)
+        cast_x(1)
+        prepare_w(0, 0)
+        weave_dz_n_pair(0, 0)
+        weave_dz_n_pair(1, 0)
+        q_dzn(0)
+        dx_scatter(0, 0)
+        gather_dy(3, 1, "dz_n0", 1)
+        form_dz(3, 1)
+        weave_dz_n_pair(0, 1)
+        weave_dz_n_pair(1, 1)
+        q_dzn(1)
+        prepare_w(1, 0)
+        dx_scatter(1, 0, "S", "dz1")
+        prepare_w(0, 1)
+        dx_scatter(0, 1)
+        store_gx(0)
+        prepare_w(1, 1)
+        dx_scatter(1, 1)
+        store_gx(1)
+        weave_dz_i(0, 0)
+        weave_dz_i(0, 1)
+        gather_x(1, 0)
+        gather_x(1, 1)
+        weave_x(0, 0, "w_raw00")
+        weave_x(0, 1, "dz0")
+        weave_dz_i(1, 0)
+        weave_dz_i(1, 1)
+        q_dzi(0)
+        q_dzi(1)
+        cast_x(2, "S", "big2")
+        dx_scatter(2, 0, "S", "big4")
+        gather_x(2, 0)
+        gather_x(2, 1)
+        cast_x(3, "S", "big3")
+        dx_scatter(2, 1, "S", "big5")
+        store_gx(2)
+        gather_x(3, 0)
+        gather_x(3, 1)
+        weave_x(1, 0)
+        q_x(0)
+        weave_x(1, 1)
+        q_x(1)
+        dx_scatter(3, 0, "S", "x_g31")
+        gw_blocks(0, 0, "w_raw00")
+        dx_scatter(3, 1, "S", "big7")
+        gw_blocks(0, 1, "w_raw10")
+        gw_blocks(1, 0, "w_raw01")
+        gw_blocks(1, 1, "w_raw11")
+        store_gx(3)

@@ -238,8 +238,9 @@ def tile_attend_gex_wx_kernel(tc, xT, dyT, hT, ts, wm, offs, out_0, out_1):
         load_x(3, "big1")
         load_w(0, 1)
         load_w(1, 1)
-        for k in range(4):
+        for k in range(2):
             nc.vector.memset(gx_win[k][:], 0.0)
+            nc.gpsimd.memset(gx_win[2 + k][:], 0.0)
         gather_h(0, 0)
         gather_h(0, 1)
         gather_ts(0)
@@ -295,21 +296,21 @@ def tile_attend_gex_wx_kernel(tc, xT, dyT, hT, ts, wm, offs, out_0, out_1):
         q_dzi(0)
         q_dzi(1)
         cast_x(2, "S", "big2")
-        dx_scatter(2, 0, "S", "big4")
         gather_x(2, 0)
-        gather_x(2, 1)
         cast_x(3, "S", "big3")
-        dx_scatter(2, 1, "S", "big5")
-        store_gx(2)
+        dx_scatter(2, 0, "S", "big4")
         gather_x(3, 0)
-        gather_x(3, 1)
         weave_x(1, 0)
         q_x(0)
+        dx_scatter(3, 0, "S", "x_g30")
+        gather_x(2, 1)
+        gather_x(3, 1)
         weave_x(1, 1)
         q_x(1)
-        dx_scatter(3, 0, "S", "x_g31")
+        dx_scatter(2, 1, "S", "x_g31")
+        store_gx(2)
         gw_blocks(0, 0, "w_raw00")
-        dx_scatter(3, 1, "S", "big7")
+        dx_scatter(3, 1, "S", "x_i0x")
         gw_blocks(0, 1, "w_raw10")
         gw_blocks(1, 0, "w_raw01")
         gw_blocks(1, 1, "w_raw11")

from contextlib import ExitStack

import concourse.mybir as mybir
from concourse.masks import make_identity

B, N, T, D, DV = 2, 512, 2048, 512, 512
FLOPS = 2 * B * N * D * DV * 2
BYTES = 4 * (D * T + 2 * DV * T + T + B * DV * D + B * D * DV + D * T) + 2 * 128 * 64

F32 = mybir.dt.float32
BF16 = mybir.dt.bfloat16
U32 = mybir.dt.uint32
U16 = mybir.dt.uint16
U8 = mybir.dt.uint8
E4 = mybir.dt.float8_e4m3fn_x4
E5 = mybir.dt.float8_e5m2_x4
ACT = mybir.ActivationFunctionType
MULT = mybir.AluOpType.mult
ADD = mybir.AluOpType.add
MAX = mybir.AluOpType.max
P = 128


def tile_attend_gex_wx_kernel(tc, xT, dyT, hT, ts, wm, offs, out_0, out_1):
    nc = tc.nc
    with ExitStack() as ctx:
        lists = ctx.enter_context(tc.tile_pool(name="lists", bufs=1))
        sb = ctx.enter_context(tc.tile_pool(name="sb", bufs=1))
        ps = ctx.enter_context(tc.psum_pool(name="ps", bufs=1))

        def tile(cols, dtype, name, tag=None, bufs=1):
            return sb.tile([P, cols], dtype, name=name, tag=tag or name, bufs=bufs, align_bytes=64)

        def bank(index, name):
            return ps.tile([P, 512], F32, name=name, tag="bank%d" % index)

        def move(engine, dst, src):
            if engine == "S":
                nc.scalar.copy(dst, src)
            elif engine == "V":
                nc.vector.tensor_copy(dst, src)
            else:
                nc.gpsimd.tensor_scalar(dst, src, 1.0, 0.0, MULT, ADD)

        offsets = lists.tile([P, B * N // 16], U16, name="offsets")
        nc.sync.dma_start(offsets[:], offs)
        slots = [offsets[:, 32 * b : 32 * b + 32] for b in range(B)]

        ident = tile(P, F32, "ident")
        make_identity(nc, ident[:])

        h_rows = hT.rearrange("(p j) t -> j p t", j=4)
        dy_rows = dyT.rearrange("(p j) t -> j p t", j=4)
        h_win = [tile(T, F32, "h%d" % j, tag="big%d" % (2 * j)) for j in range(4)]
        dy_win = [tile(T, F32, "dy%d" % j, tag="big%d" % (2 * j + 1)) for j in range(4)]
        ts_win = tile(T, F32, "ts_win")
        gx_win = [tile(T, F32, "gx%d" % k) for k in range(4)]
        w_raw, w_q, x_raw, h_g, a_g, dz_turned, dzn_q, dzi_q, x_q, x_turned = [{} for n in range(10)]
        planes, dx_sb = {}, {}
        dz = [tile(2048, BF16, "dz%d" % b) for b in range(B)]
        dz_n = [tile(2048, BF16, "dz_n%d" % b) for b in range(B)]
        dz_i = [tile(2048, BF16, "dz_i%d" % b) for b in range(B)]
        x_i = {}
        ts2 = [tile(N, F32, "ts2_%d" % b) for b in range(B)]

        def load_ts():
            nc.sync.dma_start(ts_win[:], ts)

        def load_h(j):
            nc.sync.dma_start(h_win[j][:], h_rows[j])

        def load_dy(j):
            nc.sync.dma_start(dy_win[j][:], dy_rows[j])

        def load_w(b, half):
            w_raw[b, half] = tile(1024, F32, "w_raw%d%d" % (b, half))
            nc.sync.dma_start(
                w_raw[b, half][:].rearrange("p (j d) -> p j d", j=4),
                wm[b].rearrange("(p j) d -> p j d", j=4)[:, :, 256 * half : 256 * half + 256],
            )

        def load_x(c, tag=None):
            x_raw[c] = tile(T, F32, "x_raw%d" % c, tag=tag)
            nc.sync.dma_start(x_raw[c][:], xT[P * c : P * c + P, :])

        def quantize(src, cols, dtype, name):
            codes = tile(cols, U32, name + "_codes")
            scales = tile(cols, U8, name + "_scales")
            nc.vector.quantize_mx(out=codes[:].bitcast(dtype), scales=scales[:], in_=src[:])
            return codes, scales

        def gather_ts(b):
            nc.vector.tensor_scalar(ts2[b][:], ts_win[:].indirect(slots[b]), 2.0, 0.0, MULT, ADD)

        def prepare_w(b, half, engine="S"):
            woven = tile(1024, BF16, "w_woven%d%d" % (b, half))
            move(
                engine,
                woven[:].rearrange("p (c i j) -> p c j i", i=4, j=4),
                w_raw[b, half][:].rearrange("p (j c i) -> p c j i", j=4, i=4),
            )
            w_q[b, half] = quantize(woven, 256, E4, "w%d%d" % (b, half))

        def gather_h(j, b, tag="h_g", bufs=2):
            h_g[j, b] = tile(N, F32, "h_g%d%d" % (j, b), tag=tag, bufs=bufs)
            nc.vector.tensor_copy(h_g[j, b][:], h_win[j][:].indirect(slots[b]))

        def gather_dy(j, b, tag="a_g", bufs=2):
            a_g[j, b] = tile(N, F32, "a_g%d%d" % (j, b), tag=tag, bufs=bufs)
            nc.vector.tensor_tensor(a_g[j, b][:], dy_win[j][:].indirect(slots[b]), ts2[b][:], MULT)

        def form_dz(j, b):
            plane = dz[b][:, N * j : N * j + N]
            nc.vector.scalar_tensor_tensor(plane, h_g[j, b][:], 0.0, a_g[j, b][:], MAX, MULT)
            u, e = divmod(j, 2)
            if e == 0:
                dz_turned[u, b] = bank(2 * b + u, "dz_turned%d%d" % (u, b))
            for v in range(2):
                c0 = 256 * v + P * e
                nc.tensor.transpose(dz_turned[u, b][:, c0 : c0 + P], plane.bitcast(F32)[:, v : N // 2 : 2], ident[:])

        def weave_words(dst, turned, u, engine="S"):
            move(
                engine,
                dst[:, 1024 * u : 1024 * u + 1024].bitcast(F32).rearrange("s (c v) -> s c v", v=2),
                turned[:].rearrange("s (v c) -> s c v", v=2),
            )

        def weave_dz_i(u, b):
            weave_words(dz_i[b], dz_turned[u, b], u)

        def weave_x(u, b, tag=None):
            if u == 0:
                x_i[b] = tile(2048, BF16, "x_i%d" % b, tag=tag)
            weave_words(x_i[b], x_turned[u, b], u)

        def weave_dz_n_pair(u, b, engine="S"):
            move(
                engine,
                dz_n[b][:].rearrange("p (c i u e) -> p u c e i", i=4, u=2, e=2)[:, u],
                dz[b][:, 1024 * u : 1024 * u + 1024].rearrange("p (e c i) -> p c e i", e=2, i=4),
            )

        def weave_dz_n(b, q, engine="S", parts=2):
            move(
                engine,
                dz_n[b][:].rearrange("p (q c i j) -> p q c j i", q=parts, i=4, j=4)[:, q],
                dz[b][:].rearrange("p (j q c i) -> p q c j i", j=4, q=parts, i=4)[:, q],
            )

        def q_dzn(b):
            dzn_q[b] = quantize(dz_n[b], 512, E5, "dzn%d" % b)

        def product(acc, lhs, c0, rhs):
            nc.tensor.matmul_mx(
                out=acc[:],
                lhsT=lhs[0][:, c0 : c0 + P].bitcast(E4),
                lhsT_scale=lhs[1][:, c0 : c0 + P],
                rhs=rhs[0][:].bitcast(E5),
                rhs_scale=rhs[1][:],
                start=True,
                stop=True,
            )

        def dx_block(k, b, engine="S", tag=None):
            dx_sb[k, b] = tile(N, F32, "dx_sb%d%d" % (k, b), tag=tag)
            acc = bank(6 + k % 2, "dx%d%d" % (k, b))
            product(acc, w_q[b, k // 2], P * (k % 2), dzn_q[b])
            move(engine, dx_sb[k, b][:], acc[:])

        def scatter(k, b):
            nc.vector.tensor_copy(gx_win[k][:].indirect(slots[b]), dx_sb[k, b][:])

        def dx_scatter(k, b, engine="S", tag=None):
            dx_block(k, b, engine, tag)
            scatter(k, b)

        def store_gx(k):
            nc.sync.dma_start(out_1[P * k : P * k + P, :], gx_win[k][:])

        def cast_x(c, engine="S", tag=None):
            planes[c] = tile(T, BF16, "x_plane%d" % c, tag=tag)
            for half in range(2):
                cols = slice(1024 * half, 1024 * half + 1024)
                if engine == "S":
                    nc.scalar.activation(planes[c][:, cols], x_raw[c][:, cols], ACT.Copy)
                else:
                    nc.gpsimd.tensor_copy(planes[c][:, cols], x_raw[c][:, cols])

        def gather_x(c, b, engine="S"):
            x_g = tile(N, BF16, "x_g%d%d" % (c, b))
            if engine == "S":
                nc.scalar.activation(x_g[:], planes[c][:].indirect(slots[b]), ACT.Copy)
            else:
                nc.vector.tensor_copy(x_g[:], x_raw[c][:].indirect(slots[b]))
            u, e = divmod(c, 2)
            if e == 0:
                x_turned[u, b] = bank(4 + b, "x_turned%d%d" % (u, b))
            for v in range(2):
                c0 = 256 * v + P * e
                nc.tensor.transpose(x_turned[u, b][:, c0 : c0 + P], x_g[:].bitcast(F32)[:, v : N // 2 : 2], ident[:])

        def q_dzi(b):
            dzi_q[b] = quantize(dz_i[b], 512, E5, "dzi%d" % b)

        def q_x(b):
            x_q[b] = quantize(x_i[b], 512, E4, "x%d" % b)

        def gw_blocks(b, c2, tag, engines="SS"):
            gw = tile(2 * DV, F32, "gw_sb%d%d" % (b, c2), tag=tag)
            for c in range(2):
                acc = bank(2 * c2 + c, "gw%d%d%d" % (b, c2, c))
                product(acc, x_q[b], P * (2 * c2 + c), dzi_q[b])
                move(
                    engines[c],
                    gw[:, DV * c : DV * c + DV].rearrange("d (p j) -> d p j", j=4),
                    acc[:].rearrange("d (j p) -> d p j", j=4),
                )
            nc.scalar.dma_start(
                out_0[b, 256 * c2 : 256 * c2 + 256, :].rearrange("(c d) n -> d c n", c=2),
                gw[:].rearrange("d (c n) -> d c n", c=2),
            )

        load_h(0)
        load_ts()
        load_dy(0)
        load_x(0)
        load_h(1)
        load_dy(1)
        load_x(1)
        load_h(2)
        load_dy(2)
        load_h(3)
        load_dy(3)
        load_w(0, 0)
        load_w(1, 0)
        load_x(2, "big0")
        load_x(3, "big1")
        load_w(0, 1)
        load_w(1, 1)
        for k in range(2):
            nc.vector.memset(gx_win[k][:], 0.0)
            nc.gpsimd.memset(gx_win[2 + k][:], 0.0)
        gather_h(0, 0)
        gather_h(0, 1)
        gather_ts(0)
        gather_ts(1)
        for j in range(2):
            if j > 0:
                gather_h(j, 0)
                gather_h(j, 1)
            gather_dy(j, 0)
            gather_dy(j, 1)
            form_dz(j, 0)
            form_dz(j, 1)
        gather_h(2, 0)
        gather_h(2, 1, "h_g21", 1)
        gather_dy(2, 0)
        form_dz(2, 0)
        gather_h(3, 0)
        gather_h(3, 1)
        gather_dy(3, 0)
        form_dz(3, 0)
        gather_dy(2, 1, "ts2_0", 1)
        form_dz(2, 1)
        cast_x(0)
        gather_x(0, 0)
        gather_x(0, 1)
        cast_x(1)
        prepare_w(0, 0)
        weave_dz_n_pair(0, 0)
        weave_dz_n_pair(1, 0)
        q_dzn(0)
        dx_scatter(0, 0)
        gather_dy(3, 1, "dz_n0", 1)
        form_dz(3, 1)
        weave_dz_n_pair(0, 1)
        weave_dz_n_pair(1, 1)
        q_dzn(1)
        prepare_w(1, 0)
        dx_scatter(1, 0, "S", "dz1")
        prepare_w(0, 1)
        dx_scatter(0, 1)
        store_gx(0)
        prepare_w(1, 1)
        dx_scatter(1, 1)
        store_gx(1)
        weave_dz_i(0, 0)
        weave_dz_i(0, 1)
        gather_x(1, 0)
        gather_x(1, 1)
        weave_x(0, 0, "w_raw00")
        weave_x(0, 1, "dz0")
        weave_dz_i(1, 0)
        weave_dz_i(1, 1)
        q_dzi(0)
        q_dzi(1)
        cast_x(2, "S", "big2")
        gather_x(2, 0)
        cast_x(3, "S", "big3")
        dx_scatter(2, 0, "S", "big4")
        gather_x(3, 0)
        weave_x(1, 0)
        q_x(0)
        dx_scatter(3, 0, "S", "x_g30")
        gather_x(2, 1)
        gather_x(3, 1)
        weave_x(1, 1)
        q_x(1)
        dx_scatter(2, 1, "S", "x_g31")
        store_gx(2)
        gw_blocks(0, 0, "w_raw00")
        dx_scatter(3, 1, "S", "x_i0x")
        gw_blocks(0, 1, "w_raw10")
        gw_blocks(1, 0, "w_raw01")
        gw_blocks(1, 1, "w_raw11")
        store_gx(3)
